import numpy as np
import ml_dtypes


def mxq(x, axis, fmt="e4m3"):
    dtype, down = {"e4m3": (ml_dtypes.float8_e4m3fn, 7), "e5m2": (ml_dtypes.float8_e5m2, 14)}[fmt]
    v = np.moveaxis(np.asarray(x, np.float32).astype(ml_dtypes.bfloat16).astype(np.float64), axis, -1)
    blocks = v.reshape(v.shape[:-1] + (-1, 32))
    amax = np.abs(blocks).max(-1, keepdims=True)
    byte = np.maximum(np.where(amax > 0, np.frexp(amax)[1] - 1 + 127, 0) - down, 1)
    scale = np.exp2(byte - 127.0)
    codes = (blocks / scale).astype(np.float32).astype(dtype).astype(np.float64)
    return np.moveaxis((codes * scale).reshape(v.shape), -1, axis)


WIDE = False


def mx_kscale(k):
    if not WIDE:
        return np.ones(k)
    levels = np.array([10, -10, 5, -5, 0])
    if k % 512:
        return np.exp2(np.random.permutation(np.resize(levels, k // 32))).repeat(32)
    a = np.empty((k // 512, 16))
    for p in range(k // 512):
        a[p, :8] = np.random.permutation(np.resize(levels, 8))
        for g in range(8):
            far = levels[np.abs(levels - a[p, g]) >= 10]
            a[p, g + 8] = far[np.random.randint(len(far))]
    return np.exp2(a.ravel()).repeat(32)


def f64(x):
    return np.asarray(x).astype(np.float64)


def striped(idx):
    return np.tile(idx.reshape(-1, 16).T, (8, 1)).astype(np.uint16)


def unstriped(offs):
    return offs[:16].T.reshape(-1).astype(np.int64)


E2M1 = np.array([0.0, 0.5, 1.0, 1.5, 2.0, 3.0, 4.0, 6.0, -0.0, -0.5, -1.0, -1.5, -2.0, -3.0, -4.0, -6.0])


def pack_weight(w, fmt):
    k, n = w.shape
    w = f64(np.asarray(w, np.float32).astype(ml_dtypes.bfloat16)).reshape(k // 32, 32, n)
    amax = np.abs(w).max(1)
    if fmt == "e4m3":
        byte = np.frexp(amax)[1] - 1 + 127 - 7
    else:
        mant, ex = np.frexp(amax / 6.0)
        byte = np.where(mant > 0.5, ex, ex - 1) + 127
    byte = np.clip(np.where(amax > 0, byte, 1), 1, 254)
    scaled = (w * np.exp2(127.0 - byte)[:, None, :]).reshape(k, n).astype(np.float32)
    by_word = np.ascontiguousarray(scaled.reshape(k // 512, 128, 4, n).transpose(0, 1, 3, 2))
    if fmt == "e4m3":
        words = by_word.astype(ml_dtypes.float8_e4m3fn).view(np.uint8)
    else:
        c = by_word.astype(ml_dtypes.float4_e2m1fn).view(np.uint8) & 0xF
        words = (c[..., 0::2] | (c[..., 1::2] << 4)).reshape(k // 512, 128, 2 * n)
    return np.ascontiguousarray(words), np.ascontiguousarray(byte.astype(np.uint8).reshape(k // 512, 16, n))


def unpack_weight(words, scales, fmt):
    g, _, n = scales.shape
    words = np.ascontiguousarray(words).reshape(g, 128, n, -1)
    if fmt == "e4m3":
        vals = words.view(ml_dtypes.float8_e4m3fn).astype(np.float64)
    else:
        nib = np.empty((g, 128, n, 4), np.uint8)
        nib[..., 0::2] = words & 0xF
        nib[..., 1::2] = words >> 4
        vals = E2M1[nib]
    vals = vals * np.repeat(np.exp2(scales.astype(np.float64) - 127.0), 8, axis=1)[..., None]
    return vals.transpose(0, 1, 3, 2).reshape(g * 512, n)


K, T, E, C, N = 128, 1024, 12, 256, 1024
TOP = 3


def by_expert(wq, xq):
    return np.concatenate([wq[e].T @ xq[:, e * C:(e + 1) * C] for e in range(E)], axis=1)


def setup_inputs():
    n = np.random.standard_normal
    s = mx_kscale(N)[:, None]
    deal = np.repeat(np.arange(E), C).reshape(TOP, T)[:, np.random.permutation(T)]
    deal = np.take_along_axis(deal, np.argsort(np.random.rand(TOP, T), axis=0), axis=0)
    for _ in range(8):
        s_, t_ = np.random.permutation(T).reshape(2, -1); r = np.random.randint(TOP, size=T // 2); x, y = deal[r, s_].copy(), deal[r, t_].copy()
        ok = ~((deal[:, s_] == y).any(0) | (deal[:, t_] == x).any(0)); deal[r[ok], s_[ok]] = y[ok]; deal[r[ok], t_[ok]] = x[ok]
    order = np.lexsort((np.random.rand(TOP * T), deal.reshape(-1)))
    slot_token = order % T; pos = np.empty(TOP * T, np.int64); pos[order] = np.arange(TOP * T); pos = pos.reshape(TOP, T)
    g = np.random.uniform(0.5, 1.5, (TOP, T)); g = g / g.sum(0)
    w_slot = np.empty(E * C)
    for r in range(TOP): w_slot[pos[r]] = g[r]
    dy = pack_weight(n((N, T)) * s, "e4m3")
    return {
        "dy_words": dy[0],
        "dy_scales": dy[1],
        "w": (n((E, N, K)) / np.sqrt(N) / s[None]).astype(np.float32),
        "gate": np.tile(w_slot, (K, 1)).astype(np.float32),
        "offs": striped(slot_token),
        "pos1": striped(pos[0]),
        "pos2": striped(pos[1]),
        "pos3": striped(pos[2]),
    }


def reference(dy_words, dy_scales, w, gate, offs, pos1, pos2, pos3):
    idx = unstriped(offs)
    gq = unpack_weight(dy_words, dy_scales, "e4m3")[:, idx]
    dx = f64(gate) * by_expert(mxq(f64(w), 1, "e4m3"), gq)
    return dx[:, unstriped(pos1)] + dx[:, unstriped(pos2)] + dx[:, unstriped(pos3)]

@@ -1,0 +1,194 @@
+from contextlib import ExitStack
+
+import concourse.mybir as mybir
+from concourse.masks import make_identity
+
+K, T, E, C, N = 128, 1024, 12, 256, 1024
+S = E * C
+FLOPS = 2 * S * N * K
+
+F32 = mybir.dt.float32
+BF16 = mybir.dt.bfloat16
+I32 = mybir.dt.int32
+U32 = mybir.dt.uint32
+U16 = mybir.dt.uint16
+U8 = mybir.dt.uint8
+FP8X4 = mybir.dt.float8_e4m3fn_x4
+MULT = mybir.AluOpType.mult
+ADD = mybir.AluOpType.add
+COPY = mybir.ActivationFunctionType.Copy
+
+P = 128
+PASSES = 2
+PAIR = 2 * C
+TURNED = 5
+SPLIT = (9, 11)
+ST = TURNED * PAIR
+A = 64
+
+
+def tile_moe_bdx_lin_none_kernel(
+    tc, dy_words, dy_scales, w, gate, offs, pos1, pos2, pos3, out
+):
+    nc = tc.nc
+    with ExitStack() as ctx:
+        keep = ctx.enter_context(tc.tile_pool(name="keep", bufs=1))
+        psum = ctx.enter_context(tc.psum_pool(name="psum", bufs=1))
+
+        offs_sb = keep.tile([P, S // 16], U16, name="offs_sb")
+        pos_sb = [keep.tile([P, T // 16], U16, name="pos%d_sb" % r) for r in range(3)]
+        words = [keep.tile([P, T], I32, name="words%d" % o) for o in range(PASSES)]
+        scale_rows = keep.tile([P, T], U8, name="scale_rows")
+        parts = [(e, o, 1) for e in SPLIT for o in range(PASSES)] + [(e, 0, PASSES) for e in range(E) if e not in SPLIT]
+        parts = sorted(parts)
+        raw = {}
+        for e, o, n in parts:
+            tag = "raw%d" % e if n == PASSES else "raw%d_%d" % (e, o)
+            raw[(e, o)] = keep.tile([P, n, 4, K], F32, name=tag, tag=tag, align_bytes=A)
+        gate_rows = keep.tile([P, P], F32, name="gate_rows")
+        gate_cols = keep.tile([P, ST // P], F32, name="gate_cols")
+        gate_wide = keep.tile([P, S - ST], F32, name="gate_wide")
+        ident = keep.tile([P, P], F32, name="ident")
+        dx = keep.tile([P, S], F32, name="dx")
+
+        nc.gpsimd.memset(scale_rows[:].bitcast(I32), 0)
+        nc.gpsimd.memset(gate_rows[:], 0.0)
+        make_identity(nc, ident[:])
+
+        def load_words(o):
+            nc.sync.dma_start(words[o][:], dy_words[o].rearrange("p t d -> p (t d)").bitcast(I32))
+
+        def load_w(e):
+            for e2, o, n in parts:
+                if e2 == e:
+                    rows = w[e, 512 * o : 512 * (o + n), :]
+                    nc.sync.dma_start(raw[(e, o)][:], rows.rearrange("(o p j) k -> p o j k", o=n, j=4))
+
+        nc.sync.dma_start(offs_sb[:], offs)
+        for q in range(4):
+            nc.sync.dma_start(
+                scale_rows[32 * q : 32 * q + 8, :].bitcast(I32), dy_scales[:, 4 * q : 4 * q + 4, :].bitcast(I32)
+            )
+        load_words(0)
+        load_w(0)
+        load_w(1)
+        load_words(1)
+        nc.sync.dma_start(gate_rows[0 : ST // P, :], gate[0, 0:ST].rearrange("(b p) -> b p", p=P))
+        for e in range(2, E):
+            load_w(e)
+        nc.sync.dma_start(gate_wide[:], gate[:, ST:S])
+        for tile, lst in zip(pos_sb, (pos1, pos2, pos3)):
+            nc.sync.dma_start(tile[:], lst)
+
+        turned_gate = psum.tile([P, PAIR], F32, name="turned_gate", tag="turn1")
+        nc.tensor.transpose(turned_gate[:, 0:P], gate_rows[:], ident[:])
+        nc.scalar.copy(gate_cols[:], turned_gate[:, 0 : ST // P])
+
+        w_bf = [keep.tile([P, 2, PASSES * K * 4], BF16, name="w_bf%d" % c, align_bytes=A) for c in range(E // 2)]
+        w_codes = [keep.tile([P, 2 * PASSES * K], U32, name="w_codes%d" % c, align_bytes=A) for c in range(E // 2)]
+        w_scales = [keep.tile([P, 2 * PASSES * K], U8, name="w_scales%d" % c, align_bytes=A) for c in range(E // 2)]
+        for e, o, n in parts:
+            nc.scalar.copy(
+                w_bf[e // 2][:, e % 2, 512 * o : 512 * (o + n)].rearrange("p (o c i j) -> p o c j i", o=n, i=4, j=4),
+                raw[(e, o)][:].rearrange("p o j (c i) -> p o c j i", i=4),
+            )
+
+        def quantise(c):
+            nc.vector.quantize_mx(
+                out=w_codes[c][:].bitcast(FP8X4), scales=w_scales[c][:], in_=w_bf[c][:].rearrange("p e x -> p (e x)")
+            )
+
+        def gather_words(dst, o, lo, hi):
+            nc.vector.tensor_copy(dst, words[o][:].bitcast(U32).indirect(offs_sb[:, lo // 16 : hi // 16]))
+
+        def gather_scales(dst, lo, hi):
+            nc.vector.tensor_copy(dst, scale_rows[:].indirect(offs_sb[:, lo // 16 : hi // 16]))
+
+        def w_operand(e, o):
+            cols = slice(((e % 2) * PASSES + o) * K, ((e % 2) * PASSES + o + 1) * K)
+            return w_codes[e // 2][:, cols].bitcast(FP8X4), w_scales[e // 2][:, cols]
+
+        EARLY = 3 * PAIR
+        gw_a = [keep.tile([P, EARLY], U32, name="gw_a%d" % o, align_bytes=A) for o in range(PASSES)]
+        gs_a = keep.tile([P, EARLY], U8, name="gs_a", align_bytes=A)
+        for lo in (0, 768):
+            gather_scales(gs_a[:, lo : lo + 768], lo, lo + 768)
+        for o in range(PASSES):
+            for lo in (0, 768):
+                gather_words(gw_a[o][:, lo : lo + 768], o, lo, lo + 768)
+        for c in range(3):
+            quantise(c)
+        gs_b = keep.tile([P, ST - EARLY], U8, name="gs_b", tag="raw3", align_bytes=A)
+        gw_b = {}
+        for c in range(3, TURNED):
+            cols = slice(c * PAIR - EARLY, (c + 1) * PAIR - EARLY)
+            gather_scales(gs_b[:, cols], c * PAIR, (c + 1) * PAIR)
+        for c in range(3, TURNED):
+            gw_b[c] = keep.tile([P, PASSES * PAIR], U32, name="gw_b%d" % c, tag=("raw4", "raw7")[c - 3], align_bytes=A)
+            for o in range(PASSES):
+                gather_words(gw_b[c][:, o * PAIR : (o + 1) * PAIR], o, c * PAIR, (c + 1) * PAIR)
+            quantise(c)
+        gated_tag = ["raw6", "raw8", "raw9_0", "raw11_0", "raw9_0"]
+        for c in range(TURNED):
+            gs, base = (gs_a, 0) if c < 3 else (gs_b, EARLY)
+            acc = psum.tile([P, PAIR], F32, name="acc%d" % c, tag="acc%d" % c)
+            for b in range(4):
+                slots = slice(c * PAIR + b * P - base, c * PAIR + (b + 1) * P - base)
+                for o in range(PASSES):
+                    codes, scales = w_operand(2 * c + b // 2, o)
+                    nc.tensor.matmul_mx(
+                        out=acc[:, b * P : (b + 1) * P],
+                        lhsT=(gw_a[o][:, slots] if c < 3 else gw_b[c][:, o * PAIR + b * P : o * PAIR + (b + 1) * P]).bitcast(FP8X4),
+                        lhsT_scale=gs[4 * o : P, slots],
+                        rhs=codes,
+                        rhs_scale=scales,
+                        start=(o == 0),
+                        stop=(o == PASSES - 1),
+                    )
+            gated = keep.tile([P, PAIR], F32, name="gated%d" % c, tag=gated_tag[c], align_bytes=A)
+            for b in range(4):
+                nc.scalar.activation(
+                    gated[:, b * P : (b + 1) * P], acc[:, b * P : (b + 1) * P], COPY,
+                    scale=gate_cols[:, 4 * c + b : 4 * c + b + 1],
+                )
+            turned = psum.tile([P, PAIR], F32, name="turned%d" % c, tag="turn%d" % (c % 2))
+            for b in range(4):
+                nc.tensor.transpose(turned[:, b * P : (b + 1) * P], gated[:, b * P : (b + 1) * P], ident[:])
+            nc.scalar.copy(dx[:, c * PAIR : (c + 1) * PAIR], turned[:])
+
+        gs5 = keep.tile([P, PAIR], U8, name="gs5", tag="raw9_1", align_bytes=A)
+        gw50 = keep.tile([P, PAIR], U32, name="gw50", tag="raw10", align_bytes=A)
+        gw51 = keep.tile([P, PAIR], U32, name="gw51", tag="raw11_1", align_bytes=A)
+        gather_scales(gs5[:], ST, S)
+        gather_words(gw50[:], 0, ST, S)
+        quantise(5)
+        for h in range(2):
+            gather_words(gw51[:, h * C : (h + 1) * C], 1, ST + h * C, ST + (h + 1) * C)
+        acc5 = [psum.tile([P, PAIR], F32, name="acc5%d" % h, tag=("acc4", "turn1")[h]) for h in range(2)]
+        for o in range(PASSES):
+            for h in range(2):
+                codes, scales = w_operand(10 + h, o)
+                nc.tensor.matmul_mx(
+                    out=acc5[h][:, 0:C], lhsT=codes, lhsT_scale=scales,
+                    rhs=(gw50, gw51)[o][:, h * C : (h + 1) * C].bitcast(FP8X4),
+                    rhs_scale=gs5[4 * o : P, h * C : (h + 1) * C],
+                    start=(o == 0), stop=(o == PASSES - 1),
+                )
+        for h in range(2):
+            lo = h * C
+            nc.vector.tensor_tensor(dx[:, ST + lo : ST + lo + C], acc5[h][:, 0:C], gate_wide[:, lo : lo + C], MULT)
+
+        one = keep.tile([P, T], F32, name="one")
+        two = keep.tile([P, T], F32, name="two")
+        three = keep.tile([P, T], F32, name="three")
+        for lo in range(0, T, 512):
+            nc.vector.tensor_copy(one[:, lo : lo + 512], dx[:].indirect(pos_sb[0][:, lo // 16 : (lo + 512) // 16]))
+        for lo in range(0, T, 512):
+            nc.vector.tensor_tensor(
+                two[:, lo : lo + 512], dx[:].indirect(pos_sb[1][:, lo // 16 : (lo + 512) // 16]), one[:, lo : lo + 512], ADD
+            )
+        for lo, hi in ((0, 384), (384, 640), (640, 896), (896, T)):
+            nc.vector.tensor_tensor(
+                three[:, lo:hi], dx[:].indirect(pos_sb[2][:, lo // 16 : hi // 16]), two[:, lo:hi], ADD
+            )
+            nc.sync.dma_start(out[:, lo:hi], three[:, lo:hi])

@@ -22,7 +22,7 @@ P = 128
 PASSES = 2
 PAIR = 2 * C
 TURNED = 5
-SPLIT = (9, 11)
+SPLIT = ()
 ST = TURNED * PAIR
 A = 64
 
@@ -73,25 +73,30 @@ def tile_moe_bdx_lin_none_kernel(
         load_w(0)
         load_w(1)
         load_words(1)
-        nc.sync.dma_start(gate_rows[0 : ST // P, :], gate[0, 0:ST].rearrange("(b p) -> b p", p=P))
+        for lo, hi in ((0, 16), (16, ST // P)):
+            nc.sync.dma_start(gate_rows[lo:hi, :], gate[0, lo * P : hi * P].rearrange("(b p) -> b p", p=P))
         for e in range(2, E):
             load_w(e)
         nc.sync.dma_start(gate_wide[:], gate[:, ST:S])
         for tile, lst in zip(pos_sb, (pos1, pos2, pos3)):
             nc.sync.dma_start(tile[:], lst)
 
-        turned_gate = psum.tile([P, PAIR], F32, name="turned_gate", tag="turn1")
+        banks = [psum.tile([P, PAIR], F32, name="bank%d" % b) for b in range(5)]
+        turned_gate = banks[4]
         nc.tensor.transpose(turned_gate[:, 0:P], gate_rows[:], ident[:])
         nc.scalar.copy(gate_cols[:], turned_gate[:, 0 : ST // P])
 
         w_bf = [keep.tile([P, 2, PASSES * K * 4], BF16, name="w_bf%d" % c, align_bytes=A) for c in range(E // 2)]
         w_codes = [keep.tile([P, 2 * PASSES * K], U32, name="w_codes%d" % c, align_bytes=A) for c in range(E // 2)]
         w_scales = [keep.tile([P, 2 * PASSES * K], U8, name="w_scales%d" % c, align_bytes=A) for c in range(E // 2)]
-        for e, o, n in parts:
+        def cast(e, o, n):
             nc.scalar.copy(
                 w_bf[e // 2][:, e % 2, 512 * o : 512 * (o + n)].rearrange("p (o c i j) -> p o c j i", o=n, i=4, j=4),
                 raw[(e, o)][:].rearrange("p o j (c i) -> p o c j i", i=4),
             )
+
+        for e in range(8):
+            cast(e, 0, PASSES)
 
         def quantise(c):
             nc.vector.quantize_mx(
@@ -118,20 +123,23 @@ def tile_moe_bdx_lin_none_kernel(
                 gather_words(gw_a[o][:, lo : lo + 768], o, lo, lo + 768)
         for c in range(3):
             quantise(c)
-        gs_b = keep.tile([P, ST - EARLY], U8, name="gs_b", tag="raw3", align_bytes=A)
+        gs_b = keep.tile([P, 2 * PAIR], U8, name="gs_b", tag="raw5", align_bytes=A)
         gw_b = {}
-        for c in range(3, TURNED):
+        for c in range(3, 5):
             cols = slice(c * PAIR - EARLY, (c + 1) * PAIR - EARLY)
             gather_scales(gs_b[:, cols], c * PAIR, (c + 1) * PAIR)
-        for c in range(3, TURNED):
-            gw_b[c] = keep.tile([P, PASSES * PAIR], U32, name="gw_b%d" % c, tag=("raw4", "raw7")[c - 3], align_bytes=A)
+        def late_pair(c):
+            gw_b[c] = keep.tile([P, PASSES * PAIR], U32, name="gw_b%d" % c, tag=("raw6", "raw7")[c - 3], align_bytes=A)
             for o in range(PASSES):
                 gather_words(gw_b[c][:, o * PAIR : (o + 1) * PAIR], o, c * PAIR, (c + 1) * PAIR)
             quantise(c)
-        gated_tag = ["raw6", "raw8", "raw9_0", "raw11_0", "raw9_0"]
+
+        late_pair(3)
         for c in range(TURNED):
+            if c == 4:
+                late_pair(4)
             gs, base = (gs_a, 0) if c < 3 else (gs_b, EARLY)
-            acc = psum.tile([P, PAIR], F32, name="acc%d" % c, tag="acc%d" % c)
+            acc = banks[min(c, 2)]
             for b in range(4):
                 slots = slice(c * PAIR + b * P - base, c * PAIR + (b + 1) * P - base)
                 for o in range(PASSES):
@@ -145,35 +153,40 @@ def tile_moe_bdx_lin_none_kernel(
                         start=(o == 0),
                         stop=(o == PASSES - 1),
                     )
-            gated = keep.tile([P, PAIR], F32, name="gated%d" % c, tag=gated_tag[c], align_bytes=A)
+            gated = raw[(7 + c if c < 4 else 0, 0)][:, 0].rearrange("p j k -> p (j k)")
             for b in range(4):
                 nc.scalar.activation(
                     gated[:, b * P : (b + 1) * P], acc[:, b * P : (b + 1) * P], COPY,
                     scale=gate_cols[:, 4 * c + b : 4 * c + b + 1],
                 )
-            turned = psum.tile([P, PAIR], F32, name="turned%d" % c, tag="turn%d" % (c % 2))
+            if c < 4:
+                cast(8 + c, 0, PASSES)
+            turned = banks[3 + c % 2]
             for b in range(4):
                 nc.tensor.transpose(turned[:, b * P : (b + 1) * P], gated[:, b * P : (b + 1) * P], ident[:])
             nc.scalar.copy(dx[:, c * PAIR : (c + 1) * PAIR], turned[:])
 
-        gs5 = keep.tile([P, PAIR], U8, name="gs5", tag="raw9_1", align_bytes=A)
+        def straight(acc, e, o, codes_g, scales_g):
+            codes, scales = w_operand(e, o)
+            nc.tensor.matmul_mx(
+                out=acc, lhsT=codes, lhsT_scale=scales, rhs=codes_g.bitcast(FP8X4), rhs_scale=scales_g,
+                start=(o == 0), stop=(o == PASSES - 1),
+            )
+
+        LAST = S - PAIR
+        gs5 = keep.tile([P, PAIR], U8, name="gs5", tag="raw9", align_bytes=A)
         gw50 = keep.tile([P, PAIR], U32, name="gw50", tag="raw10", align_bytes=A)
-        gw51 = keep.tile([P, PAIR], U32, name="gw51", tag="raw11_1", align_bytes=A)
-        gather_scales(gs5[:], ST, S)
-        gather_words(gw50[:], 0, ST, S)
+        gw51 = keep.tile([P, PAIR], U32, name="gw51", tag="raw11", align_bytes=A)
+        gather_scales(gs5[:], LAST, S)
+        gather_words(gw50[:], 0, LAST, S)
         quantise(5)
         for h in range(2):
-            gather_words(gw51[:, h * C : (h + 1) * C], 1, ST + h * C, ST + (h + 1) * C)
-        acc5 = [psum.tile([P, PAIR], F32, name="acc5%d" % h, tag=("acc4", "turn1")[h]) for h in range(2)]
-        for o in range(PASSES):
-            for h in range(2):
-                codes, scales = w_operand(10 + h, o)
-                nc.tensor.matmul_mx(
-                    out=acc5[h][:, 0:C], lhsT=codes, lhsT_scale=scales,
-                    rhs=(gw50, gw51)[o][:, h * C : (h + 1) * C].bitcast(FP8X4),
-                    rhs_scale=gs5[4 * o : P, h * C : (h + 1) * C],
-                    start=(o == 0), stop=(o == PASSES - 1),
-                )
+            gather_words(gw51[:, h * C : (h + 1) * C], 1, LAST + h * C, LAST + (h + 1) * C)
+        acc5 = [banks[2], banks[3]]
+        for h in range(2):
+            for o in range(PASSES):
+                straight(acc5[h][:, 0:C], 10 + h, o, (gw50, gw51)[o][:, h * C : (h + 1) * C],
+                         gs5[4 * o : P, h * C : (h + 1) * C])
         for h in range(2):
             lo = h * C
             nc.vector.tensor_tensor(dx[:, ST + lo : ST + lo + C], acc5[h][:, 0:C], gate_wide[:, lo : lo + C], MULT)

@@ -65,11 +65,11 @@ def tile_moe_bdx_lin_none_kernel(
                     nc.sync.dma_start(raw[(e, o)][:], rows.rearrange("(o p j) k -> p o j k", o=n, j=4))
 
         nc.sync.dma_start(offs_sb[:], offs)
+        load_words(0)
         for q in range(4):
             nc.sync.dma_start(
                 scale_rows[32 * q : 32 * q + 8, :].bitcast(I32), dy_scales[:, 4 * q : 4 * q + 4, :].bitcast(I32)
             )
-        load_words(0)
         load_w(0)
         load_w(1)
         load_words(1)
@@ -117,10 +117,11 @@ def tile_moe_bdx_lin_none_kernel(
         gw_a = [keep.tile([P, EARLY], U32, name="gw_a%d" % o, align_bytes=A) for o in range(PASSES)]
         gs_a = keep.tile([P, EARLY], U8, name="gs_a", align_bytes=A)
         for lo in (0, 768):
+            gather_words(gw_a[0][:, lo : lo + 768], 0, lo, lo + 768)
+        for lo in (0, 768):
             gather_scales(gs_a[:, lo : lo + 768], lo, lo + 768)
-        for o in range(PASSES):
-            for lo in (0, 768):
-                gather_words(gw_a[o][:, lo : lo + 768], o, lo, lo + 768)
+        for lo in (0, 768):
+            gather_words(gw_a[1][:, lo : lo + 768], 1, lo, lo + 768)
         for c in range(3):
             quantise(c)
         gs_b = keep.tile([P, 2 * PAIR], U8, name="gs_b", tag="raw5", align_bytes=A)

from contextlib import ExitStack

import concourse.mybir as mybir
from concourse.masks import make_identity

K, T, E, C, N = 128, 1024, 12, 256, 1024
S = E * C
FLOPS = 2 * S * N * K

F32 = mybir.dt.float32
BF16 = mybir.dt.bfloat16
I32 = mybir.dt.int32
U32 = mybir.dt.uint32
U16 = mybir.dt.uint16
U8 = mybir.dt.uint8
FP8X4 = mybir.dt.float8_e4m3fn_x4
MULT = mybir.AluOpType.mult
ADD = mybir.AluOpType.add
COPY = mybir.ActivationFunctionType.Copy

P = 128
PASSES = 2
PAIR = 2 * C
TURNED = 5
SPLIT = ()
ST = TURNED * PAIR
A = 64


def tile_moe_bdx_lin_none_kernel(
    tc, dy_words, dy_scales, w, gate, offs, pos1, pos2, pos3, out
):
    nc = tc.nc
    with ExitStack() as ctx:
        keep = ctx.enter_context(tc.tile_pool(name="keep", bufs=1))
        psum = ctx.enter_context(tc.psum_pool(name="psum", bufs=1))

        offs_sb = keep.tile([P, S // 16], U16, name="offs_sb")
        pos_sb = [keep.tile([P, T // 16], U16, name="pos%d_sb" % r) for r in range(3)]
        words = [keep.tile([P, T], I32, name="words%d" % o) for o in range(PASSES)]
        scale_rows = keep.tile([P, T], U8, name="scale_rows")
        parts = [(e, o, 1) for e in SPLIT for o in range(PASSES)] + [(e, 0, PASSES) for e in range(E) if e not in SPLIT]
        parts = sorted(parts)
        raw = {}
        for e, o, n in parts:
            tag = "raw%d" % e if n == PASSES else "raw%d_%d" % (e, o)
            raw[(e, o)] = keep.tile([P, n, 4, K], F32, name=tag, tag=tag, align_bytes=A)
        gate_rows = keep.tile([P, P], F32, name="gate_rows")
        gate_cols = keep.tile([P, ST // P], F32, name="gate_cols")
        gate_wide = keep.tile([P, S - ST], F32, name="gate_wide")
        ident = keep.tile([P, P], F32, name="ident")
        dx = keep.tile([P, S], F32, name="dx")

        nc.gpsimd.memset(scale_rows[:].bitcast(I32), 0)
        nc.gpsimd.memset(gate_rows[:], 0.0)
        make_identity(nc, ident[:])

        def load_words(o):
            nc.sync.dma_start(words[o][:], dy_words[o].rearrange("p t d -> p (t d)").bitcast(I32))

        def load_w(e):
            for e2, o, n in parts:
                if e2 == e:
                    rows = w[e, 512 * o : 512 * (o + n), :]
                    nc.sync.dma_start(raw[(e, o)][:], rows.rearrange("(o p j) k -> p o j k", o=n, j=4))

        nc.sync.dma_start(offs_sb[:], offs)
        load_words(0)
        for q in range(4):
            nc.sync.dma_start(
                scale_rows[32 * q : 32 * q + 8, :].bitcast(I32), dy_scales[:, 4 * q : 4 * q + 4, :].bitcast(I32)
            )
        load_w(0)
        load_w(1)
        load_words(1)
        for lo, hi in ((0, 16), (16, ST // P)):
            nc.sync.dma_start(gate_rows[lo:hi, :], gate[0, lo * P : hi * P].rearrange("(b p) -> b p", p=P))
        for e in range(2, E):
            load_w(e)
        nc.sync.dma_start(gate_wide[:], gate[:, ST:S])
        for tile, lst in zip(pos_sb, (pos1, pos2, pos3)):
            nc.sync.dma_start(tile[:], lst)

        banks = [psum.tile([P, PAIR], F32, name="bank%d" % b) for b in range(5)]
        turned_gate = banks[4]
        nc.tensor.transpose(turned_gate[:, 0:P], gate_rows[:], ident[:])
        nc.scalar.copy(gate_cols[:], turned_gate[:, 0 : ST // P])

        w_bf = [keep.tile([P, 2, PASSES * K * 4], BF16, name="w_bf%d" % c, align_bytes=A) for c in range(E // 2)]
        w_codes = [keep.tile([P, 2 * PASSES * K], U32, name="w_codes%d" % c, align_bytes=A) for c in range(E // 2)]
        w_scales = [keep.tile([P, 2 * PASSES * K], U8, name="w_scales%d" % c, align_bytes=A) for c in range(E // 2)]
        def cast(e, o, n):
            nc.scalar.copy(
                w_bf[e // 2][:, e % 2, 512 * o : 512 * (o + n)].rearrange("p (o c i j) -> p o c j i", o=n, i=4, j=4),
                raw[(e, o)][:].rearrange("p o j (c i) -> p o c j i", i=4),
            )

        for e in range(8):
            cast(e, 0, PASSES)

        def quantise(c):
            nc.vector.quantize_mx(
                out=w_codes[c][:].bitcast(FP8X4), scales=w_scales[c][:], in_=w_bf[c][:].rearrange("p e x -> p (e x)")
            )

        def gather_words(dst, o, lo, hi):
            nc.vector.tensor_copy(dst, words[o][:].bitcast(U32).indirect(offs_sb[:, lo // 16 : hi // 16]))

        def gather_scales(dst, lo, hi):
            nc.vector.tensor_copy(dst, scale_rows[:].indirect(offs_sb[:, lo // 16 : hi // 16]))

        def w_operand(e, o):
            cols = slice(((e % 2) * PASSES + o) * K, ((e % 2) * PASSES + o + 1) * K)
            return w_codes[e // 2][:, cols].bitcast(FP8X4), w_scales[e // 2][:, cols]

        EARLY = 3 * PAIR
        gw_a = [keep.tile([P, EARLY], U32, name="gw_a%d" % o, align_bytes=A) for o in range(PASSES)]
        gs_a = keep.tile([P, EARLY], U8, name="gs_a", align_bytes=A)
        for lo in (0, 768):
            gather_words(gw_a[0][:, lo : lo + 768], 0, lo, lo + 768)
        for lo in (0, 768):
            gather_scales(gs_a[:, lo : lo + 768], lo, lo + 768)
        for lo in (0, 768):
            gather_words(gw_a[1][:, lo : lo + 768], 1, lo, lo + 768)
        for c in range(3):
            quantise(c)
        gs_b = keep.tile([P, 2 * PAIR], U8, name="gs_b", tag="raw5", align_bytes=A)
        gw_b = {}
        for c in range(3, 5):
            cols = slice(c * PAIR - EARLY, (c + 1) * PAIR - EARLY)
            gather_scales(gs_b[:, cols], c * PAIR, (c + 1) * PAIR)
        def late_pair(c):
            gw_b[c] = keep.tile([P, PASSES * PAIR], U32, name="gw_b%d" % c, tag=("raw6", "raw7")[c - 3], align_bytes=A)
            for o in range(PASSES):
                gather_words(gw_b[c][:, o * PAIR : (o + 1) * PAIR], o, c * PAIR, (c + 1) * PAIR)
            quantise(c)

        late_pair(3)
        for c in range(TURNED):
            if c == 4:
                late_pair(4)
            gs, base = (gs_a, 0) if c < 3 else (gs_b, EARLY)
            acc = banks[min(c, 2)]
            for b in range(4):
                slots = slice(c * PAIR + b * P - base, c * PAIR + (b + 1) * P - base)
                for o in range(PASSES):
                    codes, scales = w_operand(2 * c + b // 2, o)
                    nc.tensor.matmul_mx(
                        out=acc[:, b * P : (b + 1) * P],
                        lhsT=(gw_a[o][:, slots] if c < 3 else gw_b[c][:, o * PAIR + b * P : o * PAIR + (b + 1) * P]).bitcast(FP8X4),
                        lhsT_scale=gs[4 * o : P, slots],
                        rhs=codes,
                        rhs_scale=scales,
                        start=(o == 0),
                        stop=(o == PASSES - 1),
                    )
            gated = raw[(7 + c if c < 4 else 0, 0)][:, 0].rearrange("p j k -> p (j k)")
            for b in range(4):
                nc.scalar.activation(
                    gated[:, b * P : (b + 1) * P], acc[:, b * P : (b + 1) * P], COPY,
                    scale=gate_cols[:, 4 * c + b : 4 * c + b + 1],
                )
            if c < 4:
                cast(8 + c, 0, PASSES)
            turned = banks[3 + c % 2]
            for b in range(4):
                nc.tensor.transpose(turned[:, b * P : (b + 1) * P], gated[:, b * P : (b + 1) * P], ident[:])
            nc.scalar.copy(dx[:, c * PAIR : (c + 1) * PAIR], turned[:])

        def straight(acc, e, o, codes_g, scales_g):
            codes, scales = w_operand(e, o)
            nc.tensor.matmul_mx(
                out=acc, lhsT=codes, lhsT_scale=scales, rhs=codes_g.bitcast(FP8X4), rhs_scale=scales_g,
                start=(o == 0), stop=(o == PASSES - 1),
            )

        LAST = S - PAIR
        gs5 = keep.tile([P, PAIR], U8, name="gs5", tag="raw9", align_bytes=A)
        gw50 = keep.tile([P, PAIR], U32, name="gw50", tag="raw10", align_bytes=A)
        gw51 = keep.tile([P, PAIR], U32, name="gw51", tag="raw11", align_bytes=A)
        gather_scales(gs5[:], LAST, S)
        gather_words(gw50[:], 0, LAST, S)
        quantise(5)
        for h in range(2):
            gather_words(gw51[:, h * C : (h + 1) * C], 1, LAST + h * C, LAST + (h + 1) * C)
        acc5 = [banks[2], banks[3]]
        for h in range(2):
            for o in range(PASSES):
                straight(acc5[h][:, 0:C], 10 + h, o, (gw50, gw51)[o][:, h * C : (h + 1) * C],
                         gs5[4 * o : P, h * C : (h + 1) * C])
        for h in range(2):
            lo = h * C
            nc.vector.tensor_tensor(dx[:, ST + lo : ST + lo + C], acc5[h][:, 0:C], gate_wide[:, lo : lo + C], MULT)

        one = keep.tile([P, T], F32, name="one")
        two = keep.tile([P, T], F32, name="two")
        three = keep.tile([P, T], F32, name="three")
        for lo in range(0, T, 512):
            nc.vector.tensor_copy(one[:, lo : lo + 512], dx[:].indirect(pos_sb[0][:, lo // 16 : (lo + 512) // 16]))
        for lo in range(0, T, 512):
            nc.vector.tensor_tensor(
                two[:, lo : lo + 512], dx[:].indirect(pos_sb[1][:, lo // 16 : (lo + 512) // 16]), one[:, lo : lo + 512], ADD
            )
        for lo, hi in ((0, 384), (384, 640), (640, 896), (896, T)):
            nc.vector.tensor_tensor(
                three[:, lo:hi], dx[:].indirect(pos_sb[2][:, lo // 16 : hi // 16]), two[:, lo:hi], ADD
            )
            nc.sync.dma_start(out[:, lo:hi], three[:, lo:hi])
